import numpy as np
import ml_dtypes


def mxq(x, axis, fmt="e4m3"):
    dtype, down = {"e4m3": (ml_dtypes.float8_e4m3fn, 7), "e5m2": (ml_dtypes.float8_e5m2, 14)}[fmt]
    v = np.moveaxis(np.asarray(x, np.float32).astype(ml_dtypes.bfloat16).astype(np.float64), axis, -1)
    blocks = v.reshape(v.shape[:-1] + (-1, 32))
    amax = np.abs(blocks).max(-1, keepdims=True)
    byte = np.maximum(np.where(amax > 0, np.frexp(amax)[1] - 1 + 127, 0) - down, 1)
    scale = np.exp2(byte - 127.0)
    codes = (blocks / scale).astype(np.float32).astype(dtype).astype(np.float64)
    return np.moveaxis((codes * scale).reshape(v.shape), -1, axis)


WIDE = False


def mx_kscale(k):
    if not WIDE:
        return np.ones(k)
    levels = np.array([30, -30])
    if k % 512:
        return np.exp2(np.random.permutation(np.resize(levels, k // 32))).repeat(32)
    a = np.empty((k // 512, 16))
    for p in range(k // 512):
        a[p, :8] = np.random.permutation(np.resize(levels, 8))
        for g in range(8):
            far = levels[np.abs(levels - a[p, g]) >= 10]
            a[p, g + 8] = far[np.random.randint(len(far))]
    return np.exp2(a.ravel()).repeat(32)


def f64(x):
    return np.asarray(x).astype(np.float64)


E2M1 = np.array([0.0, 0.5, 1.0, 1.5, 2.0, 3.0, 4.0, 6.0, -0.0, -0.5, -1.0, -1.5, -2.0, -3.0, -4.0, -6.0])


def pack_weight(w, fmt):
    k, n = w.shape
    w = f64(np.asarray(w, np.float32).astype(ml_dtypes.bfloat16)).reshape(k // 32, 32, n)
    amax = np.abs(w).max(1)
    if fmt == "e4m3":
        byte = np.frexp(amax)[1] - 1 + 127 - 7
    else:
        mant, ex = np.frexp(amax / 6.0)
        byte = np.where(mant > 0.5, ex, ex - 1) + 127
    byte = np.clip(np.where(amax > 0, byte, 1), 1, 254)
    scaled = (w * np.exp2(127.0 - byte)[:, None, :]).reshape(k, n).astype(np.float32)
    by_word = np.ascontiguousarray(scaled.reshape(k // 512, 128, 4, n).transpose(0, 1, 3, 2))
    if fmt == "e4m3":
        words = by_word.astype(ml_dtypes.float8_e4m3fn).view(np.uint8)
    else:
        c = by_word.astype(ml_dtypes.float4_e2m1fn).view(np.uint8) & 0xF
        words = (c[..., 0::2] | (c[..., 1::2] << 4)).reshape(k // 512, 128, 2 * n)
    return np.ascontiguousarray(words), np.ascontiguousarray(byte.astype(np.uint8).reshape(k // 512, 16, n))


def unpack_weight(words, scales, fmt):
    g, _, n = scales.shape
    words = np.ascontiguousarray(words).reshape(g, 128, n, -1)
    if fmt == "e4m3":
        vals = words.view(ml_dtypes.float8_e4m3fn).astype(np.float64)
    else:
        nib = np.empty((g, 128, n, 4), np.uint8)
        nib[..., 0::2] = words & 0xF
        nib[..., 1::2] = words >> 4
        vals = E2M1[nib]
    vals = vals * np.repeat(np.exp2(scales.astype(np.float64) - 127.0), 8, axis=1)[..., None]
    return vals.transpose(0, 1, 3, 2).reshape(g * 512, n)


K, N, T, S = 512, 512, 1024, 1024


def setup_inputs():
    n = np.random.standard_normal
    ft = mx_kscale(T)
    fs = mx_kscale(S)
    sap = pack_weight(n((S, K)) * fs[:, None], "e4m3")
    sbp = pack_weight(n((S, N)) / fs[:, None], "e2m1")
    return {
        "xa": (n((K, T))).astype(np.float32),
        "xb": (n((N, T))).astype(np.float32),
        "ra": (np.random.uniform(0.5, 1.5, (1, T)) * ft).astype(np.float32),
        "rb": (np.random.uniform(0.5, 1.5, (1, T)) / ft).astype(np.float32),
        "sa_words": sap[0],
        "sa_scales": sap[1],
        "sb_words": sbp[0],
        "sb_scales": sbp[1],
    }


def reference(xa, xb, ra, rb, sa_words, sa_scales, sb_words, sb_scales):
    sau = unpack_weight(sa_words, sa_scales, "e4m3")
    sbu = unpack_weight(sb_words, sb_scales, "e2m1")
    da = f64(xa) * f64(ra)
    bl = np.pad(f64(xb), ((0, 0), (1, 0)))[:, :T]
    db = bl * f64(rb)
    ta = da.T
    tb = db.T
    taq = mxq(ta, 0, "e4m3")
    tbq = mxq(tb, 0, "e5m2")
    v = taq.T @ tbq + sau.T @ sbu
    y = 0.03 * v
    return y

@@ -1,0 +1,215 @@
+from contextlib import ExitStack
+
+import concourse.mybir as mybir
+from concourse.masks import make_identity
+
+K, N, T, S = 512, 512, 1024, 1024
+FLOPS = 2 * K * N * (T + S)
+
+F32 = mybir.dt.float32
+BF16 = mybir.dt.bfloat16
+I32 = mybir.dt.int32
+U32 = mybir.dt.uint32
+U8 = mybir.dt.uint8
+E4M3 = mybir.dt.float8_e4m3fn_x4
+E5M2 = mybir.dt.float8_e5m2_x4
+E2M1 = mybir.dt.float4_e2m1fn_x4
+COPY = mybir.ActivationFunctionType.Copy
+MULT = mybir.AluOpType.mult
+
+P = 128
+PASS = 512
+PASSES = T // PASS
+TILES = K // P
+PAD = 64
+OUT_SCALE = 0.03
+
+
+def tile_mix_lagged_moments_kernel(tc, xa, xb, ra, rb, sa_words, sa_scales, sb_words, sb_scales, out):
+    nc = tc.nc
+    last = TILES - 1
+
+    with ExitStack() as ctx:
+        sb = ctx.enter_context(tc.tile_pool(name="sbuf", bufs=1))
+        ps = ctx.enter_context(tc.psum_pool(name="psum", bufs=1))
+        ctx.enter_context(tc.manual_schedule())
+
+        def sbuf(name, shape, dtype):
+            return sb.tile(shape, dtype, name=name, align_bytes=256)
+
+        def bank(tag, name, shape):
+            return ps.tile(shape, F32, name=name, tag=tag)
+
+        ident = sbuf("ident", [P, P], F32)
+        ra_cols = sbuf("ra_cols", [P, PASSES, 4], F32)
+        rb_cols = sbuf("rb_cols", [P, PASSES, 4], F32)
+        xa_sb = [sbuf("xa%d" % i, [P, T], F32) for i in range(TILES)]
+        xb_sb = [sbuf("xb%d" % i, [P, PAD + T], F32) for i in range(TILES)]
+        sa_codes = sbuf("sa_codes", [P, PASSES, 4 * K], U8)
+        sb_codes = sbuf("sb_codes", [P, PASSES, 2 * N], U8)
+        planes = sbuf("planes", [P, PASSES * (K + N)], U8)
+        sa_plane = planes[:, : PASSES * K]
+        sb_plane = planes[:, PASSES * K :]
+        warm = sbuf("warm", [P, 1], F32)
+
+        def load_weights(queue, cols, r):
+            queue.dma_start(out=cols[:], in_=r.rearrange("o (g p m) -> p (o g) m", g=PASSES, m=4))
+
+        def load_scales(plane, scales, quad):
+            rows = scales.bitcast(I32).rearrange("z q c -> q z c")
+            nc.sync.dma_start(
+                out=plane.bitcast(I32)[32 * quad : 32 * quad + 4, :].rearrange("p (z c) -> p z c", z=PASSES),
+                in_=rows[4 * quad : 4 * quad + 4],
+            )
+
+        def load_x(dst, first, src, i, halves):
+            width = T // halves
+            for h in range(halves):
+                nc.sync.dma_start(
+                    out=dst[:, first + h * width : first + (h + 1) * width],
+                    in_=src[i * P : (i + 1) * P, h * width : (h + 1) * width],
+                )
+
+        load_weights(nc.scalar, rb_cols, rb)
+        nc.vector.memset(planes[:].bitcast(I32), 0)
+        for i in range(TILES):
+            load_x(xb_sb[i], PAD, xb, i, 1)
+            load_scales(sa_plane, sa_scales, i)
+            load_scales(sb_plane, sb_scales, i)
+        make_identity(nc, ident[:])
+        for i in range(TILES):
+            nc.vector.memset(xb_sb[i][:, PAD - 1 : PAD], 0.0)
+        nc.scalar.activation(out=warm[:], in_=xb_sb[0][:, PAD - 1 : PAD], func=COPY, scale=OUT_SCALE)
+        load_weights(nc.sync, ra_cols, ra)
+        nc.sync.dma_start(out=sb_codes[:].bitcast(I32), in_=sb_words.bitcast(I32).rearrange("z p c -> p z c"))
+        nc.sync.dma_start(
+            out=sa_codes[:].bitcast(I32),
+            in_=sa_words.rearrange("z p c r -> p z (c r)").bitcast(I32),
+        )
+        for i in range(TILES):
+            load_x(xa_sb[i], 0, xa, i, 2 if i == last else 1)
+
+        def spread(cols, tags, name):
+            rows = []
+            for g in range(PASSES):
+                row = bank(tags[g], "%s%d" % (name, g), [P, PASS])
+                for m in range(4):
+                    nc.tensor.transpose(row[:, m:PASS:4], cols[:, g, m : m + 1].to_broadcast([P, P]), ident[:])
+                rows.append(row)
+            return rows
+
+        def weigh(name, x, first, row, g):
+            scaled = sbuf("%s_w%d" % (name, g), [P, PASS], BF16)
+            order = "p (b u i) -> p u b i"
+            nc.vector.tensor_tensor(
+                out=scaled[:].rearrange("p (u b i) -> p u b i", u=2, i=16),
+                in0=x[:, first + g * PASS : first + (g + 1) * PASS].rearrange(order, u=2, i=16),
+                in1=row[:].rearrange(order, u=2, i=16),
+                op=MULT,
+            )
+            return scaled
+
+        turns = []
+
+        def turn(scaled):
+            turned = bank("turn%d" % (len(turns) % 2), "turned%d" % len(turns), [P, len(scaled), 2, P])
+            turns.append(turned)
+            for g, tile in enumerate(scaled):
+                words = tile[:].bitcast(F32)
+                for u in range(2):
+                    nc.tensor.transpose(turned[:, g, u, :], words[:, u * P : (u + 1) * P], ident[:])
+            return turned
+
+        def quantize(codes, plane, grouped, fmt):
+            nc.vector.quantize_mx(out=codes.bitcast(fmt), scales=plane, in_=grouped)
+
+        rb_rows = spread(rb_cols, ["row0", "row1"], "rb_row")
+        tb_bf = sbuf("tb_bf", [P, PASSES * 4 * N], BF16)
+        tb_codes = sbuf("tb_codes", [P, PASSES * N], U32)
+        tb_plane = sbuf("tb_plane", [P, PASSES * N], U8)
+        tb_words = tb_bf[:].bitcast(F32).rearrange("p (g n u) -> p g n u", g=PASSES, u=2)
+        for j in range(TILES):
+            scaled = [weigh("xb%d" % j, xb_sb[j], PAD - 1, rb_rows[g], g) for g in range(PASSES)]
+            turned = turn(scaled)
+            nc.scalar.copy(out=tb_words[:, :, j * P : (j + 1) * P, :], in_=turned[:].rearrange("p g u n -> p g n u"))
+            if j == 2:
+                ra_rows = spread(ra_cols, ["row2", "row3"], "ra_row")
+        for lo, hi in ((0, 2 * P), (2 * P, 3 * P), (3 * P, 4 * P)):
+            for g in range(PASSES):
+                cols = slice(g * N + lo, g * N + hi)
+                quantize(tb_codes[:, cols], tb_plane[:, cols], tb_bf[:, 4 * cols.start : 4 * cols.stop], E5M2)
+
+        acc = [bank(tag, "acc%d" % i, [P, N]) for i, tag in enumerate(("acc0", "acc1", "row0", "row1"))]
+
+        def stored(i):
+            for z in range(PASSES):
+                nc.tensor.matmul_mx(
+                    out=acc[i][:],
+                    lhsT=sa_codes[:, z, 4 * i * P : 4 * (i + 1) * P].bitcast(E4M3),
+                    lhsT_scale=sa_plane[:, z * K + i * P : z * K + (i + 1) * P],
+                    rhs=sb_codes[:, z, :].bitcast(E2M1),
+                    rhs_scale=sb_plane[:, z * N : (z + 1) * N],
+                    start=(z == 0),
+                    stop=False,
+                )
+
+        def weigh_a(i):
+            return [weigh("xa%d" % i, xa_sb[i], 0, ra_rows[g], g) for g in range(PASSES)]
+
+        def regroup(name, scaled):
+            turned = turn(scaled)
+            grouped = sbuf(name + "_bf", [P, len(scaled) * 4 * P], BF16)
+            nc.scalar.copy(
+                out=grouped[:].bitcast(F32).rearrange("p (g k u) -> p g k u", k=P, u=2),
+                in_=turned[:].rearrange("p g u k -> p g k u"),
+            )
+            return grouped
+
+        def quantize_a(name, grouped):
+            width = grouped.shape[1] // 4
+            codes = sbuf(name + "_codes", [P, width], U32)
+            plane = sbuf(name + "_plane", [P, width], U8)
+            quantize(codes[:], plane[:], grouped[:], E4M3)
+            return [(codes[:, c : c + P], plane[:, c : c + P]) for c in range(0, width, P)]
+
+        def fresh(i, g, operand):
+            codes, plane = operand
+            nc.tensor.matmul_mx(
+                out=acc[i][:],
+                lhsT=codes.bitcast(E4M3),
+                lhsT_scale=plane,
+                rhs=tb_codes[:, g * N : (g + 1) * N].bitcast(E5M2),
+                rhs_scale=tb_plane[:, g * N : (g + 1) * N],
+                start=False,
+                stop=(g == PASSES - 1),
+            )
+
+        def finish(i, grouped):
+            for g, operand in enumerate(quantize_a("ta%d" % i, grouped)):
+                fresh(i, g, operand)
+
+        def store(i):
+            result = sbuf("result%d" % i, [P, N], F32)
+            if i == last:
+                nc.vector.tensor_scalar(out=result[:], in0=acc[i][:], scalar1=OUT_SCALE, scalar2=None, op0=MULT)
+            else:
+                nc.scalar.activation(out=result[:], in_=acc[i][:], func=COPY, scale=OUT_SCALE)
+            nc.sync.dma_start(out=out[i * P : (i + 1) * P, :], in_=result[:])
+
+        for i in range(last):
+            stored(i)
+        g0 = regroup("ta0", weigh_a(0))
+        stored(last)
+        g1 = regroup("ta1", weigh_a(1))
+        finish(0, g0)
+        store(0)
+        g2 = regroup("ta2", weigh_a(2))
+        finish(1, g1)
+        store(1)
+        scaled = weigh_a(last)
+        halves = [regroup("ta3_%d" % g, [scaled[g]]) for g in range(PASSES)]
+        finish(2, g2)
+        store(2)
+        for g in range(PASSES):
+            fresh(last, g, quantize_a("ta3_%d" % g, halves[g])[0])
+        store(last)

@@ -70,74 +70,78 @@ def tile_mix_lagged_moments_kernel(tc, xa, xb, ra, rb, sa_words, sa_scales, sb_w
                     in_=src[i * P : (i + 1) * P, h * width : (h + 1) * width],
                 )
 
-        load_weights(nc.scalar, rb_cols, rb)
+        load_weights(nc.sync, rb_cols, rb)
+        load_weights(nc.sync, ra_cols, ra)
         nc.vector.memset(planes[:].bitcast(I32), 0)
         for i in range(TILES):
-            load_x(xb_sb[i], PAD, xb, i, 1)
+            load_x(xb_sb[i], PAD, xb, i, 2 if i == 0 else 1)
             load_scales(sa_plane, sa_scales, i)
             load_scales(sb_plane, sb_scales, i)
         make_identity(nc, ident[:])
         for i in range(TILES):
             nc.vector.memset(xb_sb[i][:, PAD - 1 : PAD], 0.0)
         nc.scalar.activation(out=warm[:], in_=xb_sb[0][:, PAD - 1 : PAD], func=COPY, scale=OUT_SCALE)
-        load_weights(nc.sync, ra_cols, ra)
         nc.sync.dma_start(out=sb_codes[:].bitcast(I32), in_=sb_words.bitcast(I32).rearrange("z p c -> p z c"))
         nc.sync.dma_start(
             out=sa_codes[:].bitcast(I32),
             in_=sa_words.rearrange("z p c r -> p z (c r)").bitcast(I32),
         )
         for i in range(TILES):
-            load_x(xa_sb[i], 0, xa, i, 2 if i == last else 1)
+            load_x(xa_sb[i], 0, xa, i, 2)
 
         def spread(cols, tags, name):
             rows = []
             for g in range(PASSES):
                 row = bank(tags[g], "%s%d" % (name, g), [P, PASS])
                 for m in range(4):
-                    nc.tensor.transpose(row[:, m:PASS:4], cols[:, g, m : m + 1].to_broadcast([P, P]), ident[:])
+                    nc.tensor.transpose(row[:, m * P : (m + 1) * P], cols[:, g, m : m + 1].to_broadcast([P, P]), ident[:])
                 rows.append(row)
             return rows
 
-        def weigh(name, x, first, row, g):
+        def weigh(name, x, first, row, g, by_half=False):
             scaled = sbuf("%s_w%d" % (name, g), [P, PASS], BF16)
-            order = "p (b u i) -> p u b i"
-            nc.vector.tensor_tensor(
-                out=scaled[:].rearrange("p (u b i) -> p u b i", u=2, i=16),
-                in0=x[:, first + g * PASS : first + (g + 1) * PASS].rearrange(order, u=2, i=16),
-                in1=row[:].rearrange(order, u=2, i=16),
-                op=MULT,
-            )
+            dst = scaled[:].rearrange("p (u b a m) -> p b u a m", u=2, a=4, m=4)
+            src = x[:, first + g * PASS : first + (g + 1) * PASS].rearrange("p (b u a m) -> p b u a m", u=2, a=4, m=4)
+            factors = row[:].rearrange("p (m b u a) -> p b u a m", u=2, a=4, m=4)
+            if by_half:
+                for u in range(2):
+                    nc.vector.tensor_tensor(out=dst[:, :, u], in0=src[:, :, u], in1=factors[:, :, u], op=MULT)
+            else:
+                nc.vector.tensor_tensor(out=dst, in0=src, in1=factors, op=MULT)
             return scaled
 
-        turns = []
-
-        def turn(scaled):
-            turned = bank("turn%d" % (len(turns) % 2), "turned%d" % len(turns), [P, len(scaled), 2, P])
-            turns.append(turned)
+        def turn(name, tag, scaled):
+            turned = bank(tag, name, [P, len(scaled), 2, P])
             for g, tile in enumerate(scaled):
                 words = tile[:].bitcast(F32)
                 for u in range(2):
                     nc.tensor.transpose(turned[:, g, u, :], words[:, u * P : (u + 1) * P], ident[:])
-            return turned
+            return turned[:].rearrange("p g u c -> p g c u")
 
         def quantize(codes, plane, grouped, fmt):
             nc.vector.quantize_mx(out=codes.bitcast(fmt), scales=plane, in_=grouped)
 
         rb_rows = spread(rb_cols, ["row0", "row1"], "rb_row")
+        ra_rows = spread(ra_cols, ["row2", "row3"], "ra_row")
         tb_bf = sbuf("tb_bf", [P, PASSES * 4 * N], BF16)
         tb_codes = sbuf("tb_codes", [P, PASSES * N], U32)
         tb_plane = sbuf("tb_plane", [P, PASSES * N], U8)
         tb_words = tb_bf[:].bitcast(F32).rearrange("p (g n u) -> p g n u", g=PASSES, u=2)
-        for j in range(TILES):
+        for j, tag in enumerate(("acc0", "acc1", "turn0")):
             scaled = [weigh("xb%d" % j, xb_sb[j], PAD - 1, rb_rows[g], g) for g in range(PASSES)]
-            turned = turn(scaled)
-            nc.scalar.copy(out=tb_words[:, :, j * P : (j + 1) * P, :], in_=turned[:].rearrange("p g u n -> p g n u"))
-            if j == 2:
-                ra_rows = spread(ra_cols, ["row2", "row3"], "ra_row")
-        for lo, hi in ((0, 2 * P), (2 * P, 3 * P), (3 * P, 4 * P)):
+            nc.scalar.copy(out=tb_words[:, :, j * P : (j + 1) * P, :], in_=turn("tb%d" % j, tag, scaled))
+        scaled = [weigh("xb%d" % last, xb_sb[last], PAD - 1, rb_rows[g], g) for g in range(PASSES)]
+        for g, tag in enumerate(("turn1", "row0")):
+            nc.scalar.copy(out=tb_words[:, g : g + 1, last * P :, :], in_=turn("tb%d_%d" % (last, g), tag, [scaled[g]]))
+
+        def quantize_b(g, lo, hi):
+            cols = slice(g * N + lo * P, g * N + hi * P)
+            quantize(tb_codes[:, cols], tb_plane[:, cols], tb_bf[:, 4 * cols.start : 4 * cols.stop], E5M2)
+
+        for lo, hi in ((0, 2), (2, 3)):
             for g in range(PASSES):
-                cols = slice(g * N + lo, g * N + hi)
-                quantize(tb_codes[:, cols], tb_plane[:, cols], tb_bf[:, 4 * cols.start : 4 * cols.stop], E5M2)
+                quantize_b(g, lo, hi)
+        quantize_b(0, last, TILES)
 
         acc = [bank(tag, "acc%d" % i, [P, N]) for i, tag in enumerate(("acc0", "acc1", "row0", "row1"))]
 
@@ -153,15 +157,13 @@ def tile_mix_lagged_moments_kernel(tc, xa, xb, ra, rb, sa_words, sa_scales, sb_w
                     stop=False,
                 )
 
-        def weigh_a(i):
-            return [weigh("xa%d" % i, xa_sb[i], 0, ra_rows[g], g) for g in range(PASSES)]
+        def weigh_a(i, g):
+            return weigh("xa%d" % i, xa_sb[i], 0, ra_rows[g], g, by_half=(i, g) == (last, PASSES - 1))
 
-        def regroup(name, scaled):
-            turned = turn(scaled)
+        def regroup(name, tag, scaled):
             grouped = sbuf(name + "_bf", [P, len(scaled) * 4 * P], BF16)
             nc.scalar.copy(
-                out=grouped[:].bitcast(F32).rearrange("p (g k u) -> p g k u", k=P, u=2),
-                in_=turned[:].rearrange("p g u k -> p g k u"),
+                out=grouped[:].bitcast(F32).rearrange("p (g k u) -> p g k u", k=P, u=2), in_=turn(name, tag, scaled)
             )
             return grouped
 
@@ -184,32 +186,42 @@ def tile_mix_lagged_moments_kernel(tc, xa, xb, ra, rb, sa_words, sa_scales, sb_w
                 stop=(g == PASSES - 1),
             )
 
-        def finish(i, grouped):
-            for g, operand in enumerate(quantize_a("ta%d" % i, grouped)):
+        def store(i, on_vector, pieces=1):
+            result = sbuf("result%d" % i, [P, N], F32)
+            width = N // pieces
+            for c in range(0, N, width):
+                cols = slice(c, c + width)
+                if on_vector:
+                    nc.vector.tensor_scalar(
+                        out=result[:, cols], in0=acc[i][:, cols], scalar1=OUT_SCALE, scalar2=None, op0=MULT
+                    )
+                else:
+                    nc.scalar.activation(out=result[:, cols], in_=acc[i][:, cols], func=COPY, scale=OUT_SCALE)
+                nc.sync.dma_start(out=out[i * P : (i + 1) * P, cols], in_=result[:, cols])
+
+        def fresh_tile(i, operands):
+            for g, operand in enumerate(operands):
                 fresh(i, g, operand)
 
-        def store(i):
-            result = sbuf("result%d" % i, [P, N], F32)
-            if i == last:
-                nc.vector.tensor_scalar(out=result[:], in0=acc[i][:], scalar1=OUT_SCALE, scalar2=None, op0=MULT)
-            else:
-                nc.scalar.activation(out=result[:], in_=acc[i][:], func=COPY, scale=OUT_SCALE)
-            nc.sync.dma_start(out=out[i * P : (i + 1) * P, :], in_=result[:])
-
-        for i in range(last):
-            stored(i)
-        g0 = regroup("ta0", weigh_a(0))
-        stored(last)
-        g1 = regroup("ta1", weigh_a(1))
-        finish(0, g0)
-        store(0)
-        g2 = regroup("ta2", weigh_a(2))
-        finish(1, g1)
-        store(1)
-        scaled = weigh_a(last)
-        halves = [regroup("ta3_%d" % g, [scaled[g]]) for g in range(PASSES)]
-        finish(2, g2)
-        store(2)
-        for g in range(PASSES):
-            fresh(last, g, quantize_a("ta3_%d" % g, halves[g])[0])
-        store(last)
+        stored(0)
+        stored(1)
+        first = weigh_a(0, 0)
+        quantize_b(1, last, TILES)
+        g0 = regroup("ta0", "turn0", [first, weigh_a(0, 1)])
+        stored(2)
+        g1 = regroup("ta1", "turn1", [weigh_a(1, g) for g in range(PASSES)])
+        stored(3)
+        g2 = regroup("ta2", "turn0", [weigh_a(2, g) for g in range(PASSES)])
+        fresh_tile(0, quantize_a("ta0", g0))
+        scaled = [weigh_a(last, g) for g in range(PASSES)]
+        halves = [regroup("ta3_%d" % g, tag, [scaled[g]]) for g, tag in enumerate(("turn1", "row2"))]
+        q1 = quantize_a("ta1", g1)
+        q2 = quantize_a("ta2", g2)
+        store(0, True)
+        fresh_tile(1, q1)
+        store(1, False)
+        fresh_tile(2, q2)
+        q3 = [quantize_a("ta3_%d" % g, halves[g])[0] for g in range(PASSES)]
+        store(2, True)
+        fresh_tile(last, q3)
+        store(last, False, pieces=2)

@@ -18,210 +18,185 @@ COPY = mybir.ActivationFunctionType.Copy
 MULT = mybir.AluOpType.mult
 
 P = 128
-PASS = 512
+PACK = 4
+PASS = P * PACK
 PASSES = T // PASS
 TILES = K // P
+LAST = TILES - 1
+QUADS = P // 32
 PAD = 64
 OUT_SCALE = 0.03
 
 
 def tile_mix_lagged_moments_kernel(tc, xa, xb, ra, rb, sa_words, sa_scales, sb_words, sb_scales, out):
     nc = tc.nc
-    last = TILES - 1
 
     with ExitStack() as ctx:
-        sb = ctx.enter_context(tc.tile_pool(name="sbuf", bufs=1))
-        ps = ctx.enter_context(tc.psum_pool(name="psum", bufs=1))
+        sbuf_pool = ctx.enter_context(tc.tile_pool(name="sbuf", bufs=1))
+        psum_pool = ctx.enter_context(tc.psum_pool(name="psum", bufs=1))
         ctx.enter_context(tc.manual_schedule())
 
         def sbuf(name, shape, dtype):
-            return sb.tile(shape, dtype, name=name, align_bytes=256)
+            return sbuf_pool.tile(shape, dtype, name=name, align_bytes=256)
 
-        def bank(tag, name, shape):
-            return ps.tile(shape, F32, name=name, tag=tag)
+        def psum(bank, name, shape):
+            return psum_pool.tile(shape, F32, name=name, tag="bank%d" % bank)
 
         ident = sbuf("ident", [P, P], F32)
-        ra_cols = sbuf("ra_cols", [P, PASSES, 4], F32)
-        rb_cols = sbuf("rb_cols", [P, PASSES, 4], F32)
+        zero = sbuf("zero", [P, 1], F32)
+        ra_cols = sbuf("ra_cols", [P, PASSES, PACK], F32)
+        rb_cols = sbuf("rb_cols", [P, PASSES, PACK], F32)
         xa_sb = [sbuf("xa%d" % i, [P, T], F32) for i in range(TILES)]
         xb_sb = [sbuf("xb%d" % i, [P, PAD + T], F32) for i in range(TILES)]
-        sa_codes = sbuf("sa_codes", [P, PASSES, 4 * K], U8)
+        sa_codes = sbuf("sa_codes", [P, PASSES, PACK * K], U8)
         sb_codes = sbuf("sb_codes", [P, PASSES, 2 * N], U8)
-        planes = sbuf("planes", [P, PASSES * (K + N)], U8)
-        sa_plane = planes[:, : PASSES * K]
-        sb_plane = planes[:, PASSES * K :]
-        warm = sbuf("warm", [P, 1], F32)
+        stored_scales = sbuf("stored_scales", [P, PASSES * (K + N)], U8)
+        sa_scale_tile = stored_scales[:, : PASSES * K]
+        sb_scale_tile = stored_scales[:, PASSES * K :]
 
-        def load_weights(queue, cols, r):
-            queue.dma_start(out=cols[:], in_=r.rearrange("o (g p m) -> p (o g) m", g=PASSES, m=4))
-
-        def load_scales(plane, scales, quad):
-            rows = scales.bitcast(I32).rearrange("z q c -> q z c")
-            nc.sync.dma_start(
-                out=plane.bitcast(I32)[32 * quad : 32 * quad + 4, :].rearrange("p (z c) -> p z c", z=PASSES),
-                in_=rows[4 * quad : 4 * quad + 4],
-            )
-
-        def load_x(dst, first, src, i, halves):
-            width = T // halves
-            for h in range(halves):
+        for cols, r in ((rb_cols, rb), (ra_cols, ra)):
+            nc.sync.dma_start(out=cols[:], in_=r.rearrange("o (g p m) -> p (o g) m", g=PASSES, m=PACK))
+        nc.vector.memset(stored_scales[:].bitcast(I32), 0)
+        for i in range(TILES):
+            nc.sync.dma_start(out=xb_sb[i][:, PAD:], in_=xb[i * P : (i + 1) * P, :])
+            for scale_tile, scales in ((sa_scale_tile, sa_scales), (sb_scale_tile, sb_scales)):
                 nc.sync.dma_start(
-                    out=dst[:, first + h * width : first + (h + 1) * width],
-                    in_=src[i * P : (i + 1) * P, h * width : (h + 1) * width],
+                    out=scale_tile.bitcast(I32)[32 * i : 32 * i + QUADS, :].rearrange("p (z c) -> p z c", z=PASSES),
+                    in_=scales.bitcast(I32).rearrange("z q c -> q z c")[QUADS * i : QUADS * (i + 1)],
                 )
-
-        load_weights(nc.sync, rb_cols, rb)
-        load_weights(nc.sync, ra_cols, ra)
-        nc.vector.memset(planes[:].bitcast(I32), 0)
-        for i in range(TILES):
-            load_x(xb_sb[i], PAD, xb, i, 2 if i == 0 else 1)
-            load_scales(sa_plane, sa_scales, i)
-            load_scales(sb_plane, sb_scales, i)
-        make_identity(nc, ident[:])
-        for i in range(TILES):
-            nc.vector.memset(xb_sb[i][:, PAD - 1 : PAD], 0.0)
-        nc.scalar.activation(out=warm[:], in_=xb_sb[0][:, PAD - 1 : PAD], func=COPY, scale=OUT_SCALE)
         nc.sync.dma_start(out=sb_codes[:].bitcast(I32), in_=sb_words.bitcast(I32).rearrange("z p c -> p z c"))
-        nc.sync.dma_start(
-            out=sa_codes[:].bitcast(I32),
-            in_=sa_words.rearrange("z p c r -> p z (c r)").bitcast(I32),
-        )
+        nc.sync.dma_start(out=sa_codes[:].bitcast(I32), in_=sa_words.rearrange("z p c r -> p z (c r)").bitcast(I32))
         for i in range(TILES):
-            load_x(xa_sb[i], 0, xa, i, 2)
+            for g in range(PASSES):
+                tokens = slice(g * PASS, (g + 1) * PASS)
+                nc.sync.dma_start(out=xa_sb[i][:, tokens], in_=xa[i * P : (i + 1) * P, tokens])
 
-        def spread(cols, tags, name):
+        make_identity(nc, ident[:])
+        nc.vector.memset(zero[:], 0.0)
+        for i in range(TILES):
+            nc.scalar.activation(out=xb_sb[i][:, PAD - 1 : PAD], in_=zero[:], func=COPY)
+
+        def spread(name, cols, banks):
             rows = []
             for g in range(PASSES):
-                row = bank(tags[g], "%s%d" % (name, g), [P, PASS])
-                for m in range(4):
+                row = psum(banks[g], "%s%d" % (name, g), [P, PASS])
+                for m in range(PACK):
                     nc.tensor.transpose(row[:, m * P : (m + 1) * P], cols[:, g, m : m + 1].to_broadcast([P, P]), ident[:])
                 rows.append(row)
             return rows
 
-        def weigh(name, x, first, row, g, by_half=False):
-            scaled = sbuf("%s_w%d" % (name, g), [P, PASS], BF16)
-            dst = scaled[:].rearrange("p (u b a m) -> p b u a m", u=2, a=4, m=4)
-            src = x[:, first + g * PASS : first + (g + 1) * PASS].rearrange("p (b u a m) -> p b u a m", u=2, a=4, m=4)
-            factors = row[:].rearrange("p (m b u a) -> p b u a m", u=2, a=4, m=4)
+        def weigh(name, x, row, by_half=False):
+            weighted = sbuf(name, [P, PASS], BF16)
+            dst = weighted[:].rearrange("p (u b a m) -> p b u a m", u=2, a=4, m=PACK)
+            src = x.rearrange("p (b u a m) -> p b u a m", u=2, a=4, m=PACK)
+            factors = row[:].rearrange("p (m b u a) -> p b u a m", u=2, a=4, m=PACK)
             if by_half:
                 for u in range(2):
                     nc.vector.tensor_tensor(out=dst[:, :, u], in0=src[:, :, u], in1=factors[:, :, u], op=MULT)
             else:
                 nc.vector.tensor_tensor(out=dst, in0=src, in1=factors, op=MULT)
-            return scaled
+            return weighted
 
-        def turn(name, tag, scaled):
-            turned = bank(tag, name, [P, len(scaled), 2, P])
-            for g, tile in enumerate(scaled):
-                words = tile[:].bitcast(F32)
+        def regroup(name, bank, weighted, words):
+            turned = psum(bank, name, [P, len(weighted), 2, P])
+            for g, tile in enumerate(weighted):
+                pairs = tile[:].bitcast(F32)
                 for u in range(2):
-                    nc.tensor.transpose(turned[:, g, u, :], words[:, u * P : (u + 1) * P], ident[:])
-            return turned[:].rearrange("p g u c -> p g c u")
+                    nc.tensor.transpose(turned[:, g, u, :], pairs[:, u * P : (u + 1) * P], ident[:])
+            nc.scalar.copy(out=words, in_=turned[:].rearrange("p g u c -> p g c u"))
 
-        def quantize(codes, plane, grouped, fmt):
-            nc.vector.quantize_mx(out=codes.bitcast(fmt), scales=plane, in_=grouped)
+        rb_rows = spread("rb_row", rb_cols, (0, 1))
+        ra_rows = spread("ra_row", ra_cols, (2, 3))
 
-        rb_rows = spread(rb_cols, ["row0", "row1"], "rb_row")
-        ra_rows = spread(ra_cols, ["row2", "row3"], "ra_row")
-        tb_bf = sbuf("tb_bf", [P, PASSES * 4 * N], BF16)
+        tb_values = sbuf("tb_values", [P, PASSES * N * PACK], BF16)
         tb_codes = sbuf("tb_codes", [P, PASSES * N], U32)
-        tb_plane = sbuf("tb_plane", [P, PASSES * N], U8)
-        tb_words = tb_bf[:].bitcast(F32).rearrange("p (g n u) -> p g n u", g=PASSES, u=2)
-        for j, tag in enumerate(("acc0", "acc1", "turn0")):
-            scaled = [weigh("xb%d" % j, xb_sb[j], PAD - 1, rb_rows[g], g) for g in range(PASSES)]
-            nc.scalar.copy(out=tb_words[:, :, j * P : (j + 1) * P, :], in_=turn("tb%d" % j, tag, scaled))
-        scaled = [weigh("xb%d" % last, xb_sb[last], PAD - 1, rb_rows[g], g) for g in range(PASSES)]
-        for g, tag in enumerate(("turn1", "row0")):
-            nc.scalar.copy(out=tb_words[:, g : g + 1, last * P :, :], in_=turn("tb%d_%d" % (last, g), tag, [scaled[g]]))
+        tb_scales = sbuf("tb_scales", [P, PASSES * N], U8)
+        tb_words = tb_values[:].bitcast(F32).rearrange("p (g n u) -> p g n u", g=PASSES, u=2)
 
-        def quantize_b(g, lo, hi):
-            cols = slice(g * N + lo * P, g * N + hi * P)
-            quantize(tb_codes[:, cols], tb_plane[:, cols], tb_bf[:, 4 * cols.start : 4 * cols.stop], E5M2)
+        def weigh_xb(i):
+            lagged = xb_sb[i][:, PAD - 1 : PAD - 1 + T]
+            return [weigh("tb%d_%d" % (i, g), lagged[:, g * PASS : (g + 1) * PASS], rb_rows[g]) for g in range(PASSES)]
 
-        for lo, hi in ((0, 2), (2, 3)):
+        for i, bank in enumerate((4, 5, 6)):
+            regroup("tb_turned%d" % i, bank, weigh_xb(i), tb_words[:, :, i * P : (i + 1) * P, :])
+        weighted = weigh_xb(LAST)
+        for g, bank in enumerate((7, 0)):
+            regroup("tb_turned%d_%d" % (LAST, g), bank, [weighted[g]], tb_words[:, g : g + 1, LAST * P :, :])
+        for first, end in ((0, 2), (2, 3), (3, 4)):
             for g in range(PASSES):
-                quantize_b(g, lo, hi)
-        quantize_b(0, last, TILES)
+                lo, hi = g * N + first * P, g * N + end * P
+                nc.vector.quantize_mx(
+                    out=tb_codes[:, lo:hi].bitcast(E5M2), scales=tb_scales[:, lo:hi], in_=tb_values[:, PACK * lo : PACK * hi]
+                )
 
-        acc = [bank(tag, "acc%d" % i, [P, N]) for i, tag in enumerate(("acc0", "acc1", "row0", "row1"))]
+        sums = [psum(bank, "sum%d" % i, [P, N]) for i, bank in enumerate((4, 5, 0, 1))]
 
-        def stored(i):
+        def multiply_stored(i):
             for z in range(PASSES):
                 nc.tensor.matmul_mx(
-                    out=acc[i][:],
-                    lhsT=sa_codes[:, z, 4 * i * P : 4 * (i + 1) * P].bitcast(E4M3),
-                    lhsT_scale=sa_plane[:, z * K + i * P : z * K + (i + 1) * P],
+                    out=sums[i][:],
+                    lhsT=sa_codes[:, z, PACK * i * P : PACK * (i + 1) * P].bitcast(E4M3),
+                    lhsT_scale=sa_scale_tile[:, z * K + i * P : z * K + (i + 1) * P],
                     rhs=sb_codes[:, z, :].bitcast(E2M1),
-                    rhs_scale=sb_plane[:, z * N : (z + 1) * N],
+                    rhs_scale=sb_scale_tile[:, z * N : (z + 1) * N],
                     start=(z == 0),
                     stop=False,
                 )
 
-        def weigh_a(i, g):
-            return weigh("xa%d" % i, xa_sb[i], 0, ra_rows[g], g, by_half=(i, g) == (last, PASSES - 1))
+        def weigh_xa(i, g):
+            tokens = xa_sb[i][:, g * PASS : (g + 1) * PASS]
+            return weigh("ta%d_%d" % (i, g), tokens, ra_rows[g], by_half=(i, g) == (LAST, PASSES - 1))
 
-        def regroup(name, tag, scaled):
-            grouped = sbuf(name + "_bf", [P, len(scaled) * 4 * P], BF16)
-            nc.scalar.copy(
-                out=grouped[:].bitcast(F32).rearrange("p (g k u) -> p g k u", k=P, u=2), in_=turn(name, tag, scaled)
-            )
-            return grouped
+        def regroup_ta(name, bank, weighted):
+            values = sbuf(name + "_values", [P, len(weighted) * P * PACK], BF16)
+            regroup(name + "_turned", bank, weighted, values[:].bitcast(F32).rearrange("p (g k u) -> p g k u", k=P, u=2))
+            return values
 
-        def quantize_a(name, grouped):
-            width = grouped.shape[1] // 4
+        def quantize_ta(name, values):
+            width = values.shape[1] // PACK
             codes = sbuf(name + "_codes", [P, width], U32)
-            plane = sbuf(name + "_plane", [P, width], U8)
-            quantize(codes[:], plane[:], grouped[:], E4M3)
-            return [(codes[:, c : c + P], plane[:, c : c + P]) for c in range(0, width, P)]
+            scales = sbuf(name + "_scales", [P, width], U8)
+            nc.vector.quantize_mx(out=codes[:].bitcast(E4M3), scales=scales[:], in_=values[:])
+            return [(codes[:, c : c + P], scales[:, c : c + P]) for c in range(0, width, P)]
 
-        def fresh(i, g, operand):
-            codes, plane = operand
-            nc.tensor.matmul_mx(
-                out=acc[i][:],
-                lhsT=codes.bitcast(E4M3),
-                lhsT_scale=plane,
-                rhs=tb_codes[:, g * N : (g + 1) * N].bitcast(E5M2),
-                rhs_scale=tb_plane[:, g * N : (g + 1) * N],
-                start=False,
-                stop=(g == PASSES - 1),
-            )
+        def multiply_fresh(i, operands):
+            for g, (codes, scales) in enumerate(operands):
+                nc.tensor.matmul_mx(
+                    out=sums[i][:],
+                    lhsT=codes.bitcast(E4M3),
+                    lhsT_scale=scales,
+                    rhs=tb_codes[:, g * N : (g + 1) * N].bitcast(E5M2),
+                    rhs_scale=tb_scales[:, g * N : (g + 1) * N],
+                    start=False,
+                    stop=(g == PASSES - 1),
+                )
 
-        def store(i, on_vector, pieces=1):
+        def store(i):
             result = sbuf("result%d" % i, [P, N], F32)
-            width = N // pieces
-            for c in range(0, N, width):
-                cols = slice(c, c + width)
-                if on_vector:
+            width = N // 2 if i == LAST else N
+            for lo in range(0, N, width):
+                cols = slice(lo, lo + width)
+                if i % 2 == 0:
                     nc.vector.tensor_scalar(
-                        out=result[:, cols], in0=acc[i][:, cols], scalar1=OUT_SCALE, scalar2=None, op0=MULT
+                        out=result[:, cols], in0=sums[i][:, cols], scalar1=OUT_SCALE, scalar2=None, op0=MULT
                     )
                 else:
-                    nc.scalar.activation(out=result[:, cols], in_=acc[i][:, cols], func=COPY, scale=OUT_SCALE)
+                    nc.scalar.activation(out=result[:, cols], in_=sums[i][:, cols], func=COPY, scale=OUT_SCALE)
                 nc.sync.dma_start(out=out[i * P : (i + 1) * P, cols], in_=result[:, cols])
 
-        def fresh_tile(i, operands):
-            for g, operand in enumerate(operands):
-                fresh(i, g, operand)
-
-        stored(0)
-        stored(1)
-        first = weigh_a(0, 0)
-        quantize_b(1, last, TILES)
-        g0 = regroup("ta0", "turn0", [first, weigh_a(0, 1)])
-        stored(2)
-        g1 = regroup("ta1", "turn1", [weigh_a(1, g) for g in range(PASSES)])
-        stored(3)
-        g2 = regroup("ta2", "turn0", [weigh_a(2, g) for g in range(PASSES)])
-        fresh_tile(0, quantize_a("ta0", g0))
-        scaled = [weigh_a(last, g) for g in range(PASSES)]
-        halves = [regroup("ta3_%d" % g, tag, [scaled[g]]) for g, tag in enumerate(("turn1", "row2"))]
-        q1 = quantize_a("ta1", g1)
-        q2 = quantize_a("ta2", g2)
-        store(0, True)
-        fresh_tile(1, q1)
-        store(1, False)
-        fresh_tile(2, q2)
-        q3 = [quantize_a("ta3_%d" % g, halves[g])[0] for g in range(PASSES)]
-        store(2, True)
-        fresh_tile(last, q3)
-        store(last, False, pieces=2)
+        multiply_stored(0)
+        ta_values = []
+        for i in range(LAST):
+            multiply_stored(i + 1)
+            ta_values.append(regroup_ta("ta%d" % i, 6 + i % 2, [weigh_xa(i, g) for g in range(PASSES)]))
+        multiply_fresh(0, quantize_ta("ta0", ta_values[0]))
+        weighted = [weigh_xa(LAST, g) for g in range(PASSES)]
+        last_values = [regroup_ta("ta%d_%d" % (LAST, g), bank, [weighted[g]]) for g, bank in enumerate((7, 2))]
+        operands = {i: quantize_ta("ta%d" % i, ta_values[i]) for i in range(1, LAST)}
+        for i in range(1, LAST):
+            store(i - 1)
+            multiply_fresh(i, operands[i])
+        last_operands = [quantize_ta("ta%d_%d" % (LAST, g), last_values[g])[0] for g in range(PASSES)]
+        store(LAST - 1)
+        multiply_fresh(LAST, last_operands)
+        store(LAST)

from contextlib import ExitStack

import concourse.mybir as mybir
from concourse.masks import make_identity

K, N, T, S = 512, 512, 1024, 1024
FLOPS = 2 * K * N * (T + S)

F32 = mybir.dt.float32
BF16 = mybir.dt.bfloat16
I32 = mybir.dt.int32
U32 = mybir.dt.uint32
U8 = mybir.dt.uint8
E4M3 = mybir.dt.float8_e4m3fn_x4
E5M2 = mybir.dt.float8_e5m2_x4
E2M1 = mybir.dt.float4_e2m1fn_x4
COPY = mybir.ActivationFunctionType.Copy
MULT = mybir.AluOpType.mult

P = 128
PACK = 4
PASS = P * PACK
PASSES = T // PASS
TILES = K // P
LAST = TILES - 1
QUADS = P // 32
PAD = 64
OUT_SCALE = 0.03


def tile_mix_lagged_moments_kernel(tc, xa, xb, ra, rb, sa_words, sa_scales, sb_words, sb_scales, out):
    nc = tc.nc

    with ExitStack() as ctx:
        sbuf_pool = ctx.enter_context(tc.tile_pool(name="sbuf", bufs=1))
        psum_pool = ctx.enter_context(tc.psum_pool(name="psum", bufs=1))
        ctx.enter_context(tc.manual_schedule())

        def sbuf(name, shape, dtype):
            return sbuf_pool.tile(shape, dtype, name=name, align_bytes=256)

        def psum(bank, name, shape):
            return psum_pool.tile(shape, F32, name=name, tag="bank%d" % bank)

        ident = sbuf("ident", [P, P], F32)
        zero = sbuf("zero", [P, 1], F32)
        ra_cols = sbuf("ra_cols", [P, PASSES, PACK], F32)
        rb_cols = sbuf("rb_cols", [P, PASSES, PACK], F32)
        xa_sb = [sbuf("xa%d" % i, [P, T], F32) for i in range(TILES)]
        xb_sb = [sbuf("xb%d" % i, [P, PAD + T], F32) for i in range(TILES)]
        sa_codes = sbuf("sa_codes", [P, PASSES, PACK * K], U8)
        sb_codes = sbuf("sb_codes", [P, PASSES, 2 * N], U8)
        stored_scales = sbuf("stored_scales", [P, PASSES * (K + N)], U8)
        sa_scale_tile = stored_scales[:, : PASSES * K]
        sb_scale_tile = stored_scales[:, PASSES * K :]

        for cols, r in ((rb_cols, rb), (ra_cols, ra)):
            nc.sync.dma_start(out=cols[:], in_=r.rearrange("o (g p m) -> p (o g) m", g=PASSES, m=PACK))
        nc.vector.memset(stored_scales[:].bitcast(I32), 0)
        for i in range(TILES):
            nc.sync.dma_start(out=xb_sb[i][:, PAD:], in_=xb[i * P : (i + 1) * P, :])
            for scale_tile, scales in ((sa_scale_tile, sa_scales), (sb_scale_tile, sb_scales)):
                nc.sync.dma_start(
                    out=scale_tile.bitcast(I32)[32 * i : 32 * i + QUADS, :].rearrange("p (z c) -> p z c", z=PASSES),
                    in_=scales.bitcast(I32).rearrange("z q c -> q z c")[QUADS * i : QUADS * (i + 1)],
                )
        nc.sync.dma_start(out=sb_codes[:].bitcast(I32), in_=sb_words.bitcast(I32).rearrange("z p c -> p z c"))
        nc.sync.dma_start(out=sa_codes[:].bitcast(I32), in_=sa_words.rearrange("z p c r -> p z (c r)").bitcast(I32))
        for i in range(TILES):
            for g in range(PASSES):
                tokens = slice(g * PASS, (g + 1) * PASS)
                nc.sync.dma_start(out=xa_sb[i][:, tokens], in_=xa[i * P : (i + 1) * P, tokens])

        make_identity(nc, ident[:])
        nc.vector.memset(zero[:], 0.0)
        for i in range(TILES):
            nc.scalar.activation(out=xb_sb[i][:, PAD - 1 : PAD], in_=zero[:], func=COPY)

        def spread(name, cols, banks):
            rows = []
            for g in range(PASSES):
                row = psum(banks[g], "%s%d" % (name, g), [P, PASS])
                for m in range(PACK):
                    nc.tensor.transpose(row[:, m * P : (m + 1) * P], cols[:, g, m : m + 1].to_broadcast([P, P]), ident[:])
                rows.append(row)
            return rows

        def weigh(name, x, row, by_half=False):
            weighted = sbuf(name, [P, PASS], BF16)
            dst = weighted[:].rearrange("p (u b a m) -> p b u a m", u=2, a=4, m=PACK)
            src = x.rearrange("p (b u a m) -> p b u a m", u=2, a=4, m=PACK)
            factors = row[:].rearrange("p (m b u a) -> p b u a m", u=2, a=4, m=PACK)
            if by_half:
                for u in range(2):
                    nc.vector.tensor_tensor(out=dst[:, :, u], in0=src[:, :, u], in1=factors[:, :, u], op=MULT)
            else:
                nc.vector.tensor_tensor(out=dst, in0=src, in1=factors, op=MULT)
            return weighted

        def regroup(name, bank, weighted, words):
            turned = psum(bank, name, [P, len(weighted), 2, P])
            for g, tile in enumerate(weighted):
                pairs = tile[:].bitcast(F32)
                for u in range(2):
                    nc.tensor.transpose(turned[:, g, u, :], pairs[:, u * P : (u + 1) * P], ident[:])
            nc.scalar.copy(out=words, in_=turned[:].rearrange("p g u c -> p g c u"))

        rb_rows = spread("rb_row", rb_cols, (0, 1))
        ra_rows = spread("ra_row", ra_cols, (2, 3))

        tb_values = sbuf("tb_values", [P, PASSES * N * PACK], BF16)
        tb_codes = sbuf("tb_codes", [P, PASSES * N], U32)
        tb_scales = sbuf("tb_scales", [P, PASSES * N], U8)
        tb_words = tb_values[:].bitcast(F32).rearrange("p (g n u) -> p g n u", g=PASSES, u=2)

        def weigh_xb(i):
            lagged = xb_sb[i][:, PAD - 1 : PAD - 1 + T]
            return [weigh("tb%d_%d" % (i, g), lagged[:, g * PASS : (g + 1) * PASS], rb_rows[g]) for g in range(PASSES)]

        for i, bank in enumerate((4, 5, 6)):
            regroup("tb_turned%d" % i, bank, weigh_xb(i), tb_words[:, :, i * P : (i + 1) * P, :])
        weighted = weigh_xb(LAST)
        for g, bank in enumerate((7, 0)):
            regroup("tb_turned%d_%d" % (LAST, g), bank, [weighted[g]], tb_words[:, g : g + 1, LAST * P :, :])
        for first, end in ((0, 2), (2, 3), (3, 4)):
            for g in range(PASSES):
                lo, hi = g * N + first * P, g * N + end * P
                nc.vector.quantize_mx(
                    out=tb_codes[:, lo:hi].bitcast(E5M2), scales=tb_scales[:, lo:hi], in_=tb_values[:, PACK * lo : PACK * hi]
                )

        sums = [psum(bank, "sum%d" % i, [P, N]) for i, bank in enumerate((4, 5, 0, 1))]

        def multiply_stored(i):
            for z in range(PASSES):
                nc.tensor.matmul_mx(
                    out=sums[i][:],
                    lhsT=sa_codes[:, z, PACK * i * P : PACK * (i + 1) * P].bitcast(E4M3),
                    lhsT_scale=sa_scale_tile[:, z * K + i * P : z * K + (i + 1) * P],
                    rhs=sb_codes[:, z, :].bitcast(E2M1),
                    rhs_scale=sb_scale_tile[:, z * N : (z + 1) * N],
                    start=(z == 0),
                    stop=False,
                )

        def weigh_xa(i, g):
            tokens = xa_sb[i][:, g * PASS : (g + 1) * PASS]
            return weigh("ta%d_%d" % (i, g), tokens, ra_rows[g], by_half=(i, g) == (LAST, PASSES - 1))

        def regroup_ta(name, bank, weighted):
            values = sbuf(name + "_values", [P, len(weighted) * P * PACK], BF16)
            regroup(name + "_turned", bank, weighted, values[:].bitcast(F32).rearrange("p (g k u) -> p g k u", k=P, u=2))
            return values

        def quantize_ta(name, values):
            width = values.shape[1] // PACK
            codes = sbuf(name + "_codes", [P, width], U32)
            scales = sbuf(name + "_scales", [P, width], U8)
            nc.vector.quantize_mx(out=codes[:].bitcast(E4M3), scales=scales[:], in_=values[:])
            return [(codes[:, c : c + P], scales[:, c : c + P]) for c in range(0, width, P)]

        def multiply_fresh(i, operands):
            for g, (codes, scales) in enumerate(operands):
                nc.tensor.matmul_mx(
                    out=sums[i][:],
                    lhsT=codes.bitcast(E4M3),
                    lhsT_scale=scales,
                    rhs=tb_codes[:, g * N : (g + 1) * N].bitcast(E5M2),
                    rhs_scale=tb_scales[:, g * N : (g + 1) * N],
                    start=False,
                    stop=(g == PASSES - 1),
                )

        def store(i):
            result = sbuf("result%d" % i, [P, N], F32)
            width = N // 2 if i == LAST else N
            for lo in range(0, N, width):
                cols = slice(lo, lo + width)
                if i % 2 == 0:
                    nc.vector.tensor_scalar(
                        out=result[:, cols], in0=sums[i][:, cols], scalar1=OUT_SCALE, scalar2=None, op0=MULT
                    )
                else:
                    nc.scalar.activation(out=result[:, cols], in_=sums[i][:, cols], func=COPY, scale=OUT_SCALE)
                nc.sync.dma_start(out=out[i * P : (i + 1) * P, cols], in_=result[:, cols])

        multiply_stored(0)
        ta_values = []
        for i in range(LAST):
            multiply_stored(i + 1)
            ta_values.append(regroup_ta("ta%d" % i, 6 + i % 2, [weigh_xa(i, g) for g in range(PASSES)]))
        multiply_fresh(0, quantize_ta("ta0", ta_values[0]))
        weighted = [weigh_xa(LAST, g) for g in range(PASSES)]
        last_values = [regroup_ta("ta%d_%d" % (LAST, g), bank, [weighted[g]]) for g, bank in enumerate((7, 2))]
        operands = {i: quantize_ta("ta%d" % i, ta_values[i]) for i in range(1, LAST)}
        for i in range(1, LAST):
            store(i - 1)
            multiply_fresh(i, operands[i])
        last_operands = [quantize_ta("ta%d_%d" % (LAST, g), last_values[g])[0] for g in range(PASSES)]
        store(LAST - 1)
        multiply_fresh(LAST, last_operands)
        store(LAST)
